import numpy as np
import ml_dtypes


def mxq(x, axis, fmt="e4m3"):
    dtype, down = {"e4m3": (ml_dtypes.float8_e4m3fn, 7), "e5m2": (ml_dtypes.float8_e5m2, 14)}[fmt]
    v = np.moveaxis(np.asarray(x, np.float32).astype(ml_dtypes.bfloat16).astype(np.float64), axis, -1)
    blocks = v.reshape(v.shape[:-1] + (-1, 32))
    amax = np.abs(blocks).max(-1, keepdims=True)
    byte = np.maximum(np.where(amax > 0, np.frexp(amax)[1] - 1 + 127, 0) - down, 1)
    scale = np.exp2(byte - 127.0)
    codes = (blocks / scale).astype(np.float32).astype(dtype).astype(np.float64)
    return np.moveaxis((codes * scale).reshape(v.shape), -1, axis)


WIDE = False


def mx_kscale(k):
    if not WIDE:
        return np.ones(k)
    levels = np.array([10, -10, 5, -5, 0])
    if k % 512:
        return np.exp2(np.random.permutation(np.resize(levels, k // 32))).repeat(32)
    a = np.empty((k // 512, 16))
    for p in range(k // 512):
        a[p, :8] = np.random.permutation(np.resize(levels, 8))
        for g in range(8):
            far = levels[np.abs(levels - a[p, g]) >= 10]
            a[p, g + 8] = far[np.random.randint(len(far))]
    return np.exp2(a.ravel()).repeat(32)


def f64(x):
    return np.asarray(x).astype(np.float64)


def striped(idx):
    return np.tile(idx.reshape(-1, 16).T, (8, 1)).astype(np.uint16)


def unstriped(offs):
    return offs[:16].T.reshape(-1).astype(np.int64)


E2M1 = np.array([0.0, 0.5, 1.0, 1.5, 2.0, 3.0, 4.0, 6.0, -0.0, -0.5, -1.0, -1.5, -2.0, -3.0, -4.0, -6.0])


def pack_weight(w, fmt):
    k, n = w.shape
    w = f64(np.asarray(w, np.float32).astype(ml_dtypes.bfloat16)).reshape(k // 32, 32, n)
    amax = np.abs(w).max(1)
    if fmt == "e4m3":
        byte = np.frexp(amax)[1] - 1 + 127 - 7
    else:
        mant, ex = np.frexp(amax / 6.0)
        byte = np.where(mant > 0.5, ex, ex - 1) + 127
    byte = np.clip(np.where(amax > 0, byte, 1), 1, 254)
    scaled = (w * np.exp2(127.0 - byte)[:, None, :]).reshape(k, n).astype(np.float32)
    by_word = np.ascontiguousarray(scaled.reshape(k // 512, 128, 4, n).transpose(0, 1, 3, 2))
    if fmt == "e4m3":
        words = by_word.astype(ml_dtypes.float8_e4m3fn).view(np.uint8)
    else:
        c = by_word.astype(ml_dtypes.float4_e2m1fn).view(np.uint8) & 0xF
        words = (c[..., 0::2] | (c[..., 1::2] << 4)).reshape(k // 512, 128, 2 * n)
    return np.ascontiguousarray(words), np.ascontiguousarray(byte.astype(np.uint8).reshape(k // 512, 16, n))


def unpack_weight(words, scales, fmt):
    g, _, n = scales.shape
    words = np.ascontiguousarray(words).reshape(g, 128, n, -1)
    if fmt == "e4m3":
        vals = words.view(ml_dtypes.float8_e4m3fn).astype(np.float64)
    else:
        nib = np.empty((g, 128, n, 4), np.uint8)
        nib[..., 0::2] = words & 0xF
        nib[..., 1::2] = words >> 4
        vals = E2M1[nib]
    vals = vals * np.repeat(np.exp2(scales.astype(np.float64) - 127.0), 8, axis=1)[..., None]
    return vals.transpose(0, 1, 3, 2).reshape(g * 512, n)


def gelu(v):
    return 0.5 * v * (1.0 + np.tanh(np.sqrt(2.0 / np.pi) * (v + 0.044715 * v**3)))


K, T, S, H, T2, P = 1536, 4096, 1024, 1024, 2048, 512

def setup_inputs():
    n = np.random.standard_normal
    s = mx_kscale(K)[:, None]
    u = mx_kscale(H)[:, None]
    tab_words, tab_scales = pack_weight(n((K, T)) * s, "e4m3")
    w2_words, w2_scales = pack_weight(0.3 * n((H, H)) / np.sqrt(H) / u, "e2m1")
    return {
        "tab_words": tab_words,
        "tab_scales": tab_scales,
        "w1": (n((K, H)) / np.sqrt(K) / s * u.T).astype(np.float32),
        "w2_words": w2_words,
        "w2_scales": w2_scales,
        "page0": (n((H, T2)) * u).astype(np.float32),
        "least": (n((H, S)) * u).astype(np.float32),
        "phase": np.random.uniform(-1.05, 1.05, H).astype(np.float32),
        "offs": striped(np.random.permutation(T)[:S]),
        "offs2": striped(np.random.permutation(T2)[:S]),
        "offs3": striped(np.random.permutation(T2)[:P]),
    }

def reference(tab_words, tab_scales, w1, w2_words, w2_scales, page0, least, phase, offs, offs2, offs3):
    v = unpack_weight(tab_words, tab_scales, "e4m3")[:, unstriped(offs)]
    h = mxq(f64(w1), 0, "e4m3").T @ v
    page = f64(page0).copy()
    l2 = unstriped(offs2)
    page[:, l2] = np.maximum(page[:, l2] + h, f64(least))
    x = page[:, unstriped(offs3)]
    w2 = unpack_weight(w2_words, w2_scales, "e2m1")
    y = w2.T @ mxq(x, 0, "e4m3")
    return x * np.cos(y + f64(phase)[:, None])

@@ -1,0 +1,234 @@
+import math
+from contextlib import ExitStack
+
+import concourse.mybir as mybir
+
+K, T, S, H, T2, NP = 1536, 4096, 1024, 1024, 2048, 512
+FLOPS = 2 * K * H * S + 2 * H * H * NP
+
+F32 = mybir.dt.float32
+BF16 = mybir.dt.bfloat16
+I32 = mybir.dt.int32
+U32 = mybir.dt.uint32
+U16 = mybir.dt.uint16
+U8 = mybir.dt.uint8
+FP8X4 = mybir.dt.float8_e4m3fn_x4
+FP4X4 = mybir.dt.float4_e2m1fn_x4
+ALU = mybir.AluOpType
+ACT = mybir.ActivationFunctionType
+
+P = 128
+PACK = 4
+KP = P * PACK
+BANK = 512
+PASSES1 = K // KP
+PASSES2 = H // KP
+SLICES = H // P
+TWO_PI = 2.0 * math.pi
+GROUPS = ((0, 1), (2, 3), (4, 5), (6, 7))
+
+
+def tile_list_damper_record_cosine_kernel(
+    tc, tab_words, tab_scales, w1, w2_words, w2_scales, page0, least, phase, offs, offs2, offs3, out
+):
+    nc = tc.nc
+    with ExitStack() as ctx:
+        keep = ctx.enter_context(tc.tile_pool(name="keep", bufs=1))
+        work = ctx.enter_context(tc.tile_pool(name="work", bufs=2))
+        psum = ctx.enter_context(tc.psum_pool(name="psum", bufs=1))
+
+        list1 = keep.tile([P, S // 16], U16, name="list1")
+        list2 = keep.tile([P, S // 16], U16, name="list2")
+        list3 = keep.tile([P, NP // 16], U16, name="list3")
+        nc.sync.dma_start(list1[:], offs)
+
+        tscale = keep.tile([P, T], U8, name="tscale", align_bytes=64)
+        nc.vector.memset(tscale[:].bitcast(I32), 0)
+        for q in range(4):
+            nc.scalar.dma_start(
+                tscale[32 * q : 32 * q + 4 * PASSES1, :].bitcast(I32),
+                tab_scales[:, 4 * q : 4 * q + 4, :].bitcast(I32),
+            )
+
+        w1_codes = {}
+        w1_scale = {}
+
+        def load_w1(b, a):
+            raw = work.tile([P, PACK, KP], F32, name="w1raw", bufs=3)
+            nc.sync.dma_start(
+                raw[:], w1[a * KP : (a + 1) * KP, b * KP : (b + 1) * KP].rearrange("(p i) c -> p i c", i=PACK)
+            )
+            return raw
+
+        def quant_w1(b, a, raw, engine_copy):
+            grouped = work.tile([P, KP * PACK], BF16, name="w1bf", align_bytes=64)
+            engine_copy(
+                grouped[:].rearrange("p (t m i) -> p m i t", t=PACK, i=PACK),
+                raw[:].rearrange("p i (m t) -> p m i t", t=PACK),
+            )
+            codes = keep.tile([P, KP], U32, name="w1c%d%d" % (b, a), align_bytes=64)
+            scale = keep.tile([P, KP], U8, name="w1s%d%d" % (b, a), align_bytes=64)
+            nc.vector.quantize_mx(out=codes[:].bitcast(FP8X4), scales=scale[:], in_=grouped[:])
+            w1_codes[b, a] = codes
+            w1_scale[b, a] = scale
+
+        vscale = keep.tile([P, S], U8, name="vscale", align_bytes=64)
+        vwords = []
+        for a in range(PASSES1):
+            raw = load_w1(0, a)
+            table = work.tile([P, T], I32, name="big", bufs=3)
+            nc.sync.dma_start(table[:], tab_words[a].rearrange("p t i -> p (t i)").bitcast(I32))
+            quant_w1(0, a, raw, nc.vector.tensor_copy)
+            if a == 0:
+                nc.vector.tensor_copy(vscale[:], tscale[:].indirect(list1[:]))
+            halves = []
+            for u in range(2):
+                picked = keep.tile([P, BANK], U32, name="v%d%d" % (a, u), align_bytes=64)
+                nc.vector.tensor_copy(picked[:], table[:].bitcast(U32).indirect(list1[:, 32 * u : 32 * u + 32]))
+                halves.append(picked)
+            vwords.append(halves)
+            if a == 1:
+                nc.sync.dma_start(list2[:], offs2)
+                nc.sync.dma_start(list3[:], offs3)
+
+        page_rows = page0.rearrange("(b p t) c -> b t p c", p=P, t=PACK)
+
+        def bank(i):
+            return psum.tile([P, BANK], F32, name="bank%d" % i)
+
+        def make_h(s):
+            b, t = divmod(s, PACK)
+            h = work.tile([P, S], F32, name="h", bufs=3, align_bytes=64)
+            for u in range(2):
+                acc = bank(2 * (s % 2) + u)
+                for a in range(PASSES1):
+                    nc.tensor.matmul_mx(
+                        out=acc[:],
+                        lhsT=w1_codes[b, a][:, t * P : (t + 1) * P].bitcast(FP8X4),
+                        lhsT_scale=w1_scale[b, a][:, t * P : (t + 1) * P],
+                        rhs=vwords[a][u][:].bitcast(FP8X4),
+                        rhs_scale=vscale[4 * a : P, u * BANK : (u + 1) * BANK],
+                        start=(a == 0),
+                        stop=(a == PASSES1 - 1),
+                    )
+                nc.scalar.copy(h[:, u * BANK : (u + 1) * BANK], acc[:])
+            return h
+
+        x4 = [keep.tile([P, PACK, NP], F32, name="x4_%d" % b) for b in range(PASSES2)]
+        xn = []
+        x_codes = []
+        x_scale = []
+
+        def quant_x(b, engine_copy, tag):
+            grouped = work.tile([P, NP * PACK], BF16, name=tag, bufs=3, align_bytes=64)
+            engine_copy(
+                grouped[:].rearrange("p (c i t) -> p c t i", i=4, t=PACK),
+                x4[b][:].rearrange("p t (c i) -> p c t i", i=4),
+            )
+            codes = keep.tile([P, NP], U32, name="xc%d" % b, align_bytes=64)
+            scale = keep.tile([P, NP], U8, name="xs%d" % b, align_bytes=64)
+            nc.vector.quantize_mx(out=codes[:].bitcast(FP8X4), scales=scale[:], in_=grouped[:])
+            x_codes.append(codes)
+            x_scale.append(scale)
+
+        w2c = keep.tile([P, PASSES2, 2 * H], U8, name="w2c", align_bytes=64)
+        w2s = keep.tile([P, PASSES2, H], U8, name="w2s", align_bytes=64)
+        ph = keep.tile([P, SLICES], F32, name="ph")
+        shifted = keep.tile([P, SLICES], F32, name="shifted")
+
+        ybank = {}
+
+        def y_pass(m, b):
+            if b == 0:
+                ybank[m] = bank((m + 4) % 8)
+            nc.tensor.matmul_mx(
+                out=ybank[m][:],
+                lhsT=w2c[:, b, 2 * m * P : 2 * (m + 1) * P].bitcast(FP4X4),
+                lhsT_scale=w2s[:, b, m * P : (m + 1) * P],
+                rhs=x_codes[b][:].bitcast(FP8X4),
+                rhs_scale=x_scale[b][:],
+                start=(b == 0),
+                stop=(b == PASSES2 - 1),
+            )
+
+        floors = {}
+        pages = {}
+        least_by_slice = least.rearrange("(b p t) c -> p b t c", p=P, t=PACK)
+
+        def load_group(group):
+            for s in group:
+                b, t = divmod(s, PACK)
+                page = work.tile([P, T2], F32, name="page", bufs=4)
+                nc.sync.dma_start(page[:], page_rows[b, t])
+                pages[s] = page
+            b, t = divmod(group[0], PACK)
+            floor = work.tile([P, len(group), S], F32, name="floor", align_bytes=64)
+            nc.sync.dma_start(floor[:], least_by_slice[:, b, t : t + len(group), :])
+            for i, s in enumerate(group):
+                floors[s] = floor[:, i, :]
+
+        groups = GROUPS
+        load_group(groups[0])
+        load_group(groups[1])
+        for a in range(PASSES1):
+            quant_w1(1, a, load_w1(1, a), nc.scalar.copy)
+        for g, group in enumerate(groups):
+            if g == 1:
+                nc.sync.dma_start(w2c[:].bitcast(I32), w2_words.rearrange("a p c -> p a c").bitcast(I32))
+                nc.gpsimd.memset(w2s[:].bitcast(I32), 0)
+                for q in range(4):
+                    nc.sync.dma_start(
+                        w2s[32 * q : 32 * q + 4, :, :].bitcast(I32),
+                        w2_scales[:, 4 * q : 4 * q + 4, :].rearrange("a r n -> r a n").bitcast(I32),
+                    )
+                with nc.allow_non_contiguous_dma(reason="one phase value a partition"):
+                    nc.sync.dma_start(ph[:], phase.rearrange("(m p) -> p m", p=P))
+                nc.gpsimd.tensor_scalar(shifted[:], ph[:], 1.0, -math.pi, ALU.mult, ALU.add)
+            if g + 2 < len(groups):
+                load_group(groups[g + 2])
+            news = {}
+            for s in group:
+                b, t = divmod(s, PACK)
+                if t == 0:
+                    xn.append(work.tile([P, PACK, NP], F32, name="big", bufs=3))
+                h = make_h(s)
+                new = work.tile([P, S], F32, name="new", bufs=3)
+                news[s] = new
+                if s == 0:
+                    for u in range(2):
+                        cols = slice(u * BANK, (u + 1) * BANK)
+                        nc.vector.tensor_tensor(
+                            new[:, cols], pages[s][:].indirect(list2[:, 32 * u : 32 * u + 32]), h[:, cols], ALU.add
+                        )
+                else:
+                    nc.vector.tensor_tensor(new[:], pages[s][:].indirect(list2[:]), h[:], ALU.add)
+            if g == len(groups) - 1:
+                quant_x(0, nc.scalar.copy, "h")
+                for m in range(SLICES):
+                    y_pass(m, 0)
+            for s in group:
+                nc.vector.tensor_tensor(news[s][:], news[s][:], floors[s], ALU.max)
+            for s in group:
+                nc.vector.tensor_copy(pages[s][:].indirect(list2[:]), news[s][:])
+            for s in group:
+                b, t = divmod(s, PACK)
+                nc.vector.tensor_copy(x4[b][:, t, :], pages[s][:].indirect(list3[:]))
+                for q in range(4):
+                    nc.sync.dma_start(xn[b][t:P:PACK, q, :], x4[b][32 * q : 32 * q + 32, t, :])
+
+        quant_x(1, nc.vector.tensor_copy, "h")
+        for m in range(SLICES):
+            y_pass(m, 1)
+            y = ybank[m]
+            turns = work.tile([P, NP], I32, name="turns", tag="w1raw", bufs=3)
+            nc.vector.tensor_scalar(turns[:], y[:], shifted[:, m : m + 1], 1.0 / TWO_PI, ALU.add, ALU.mult)
+            rest = work.tile([P, NP], F32, name="rest", tag="page", bufs=4)
+            nc.vector.scalar_tensor_tensor(rest[:], turns[:], -TWO_PI, y[:], ALU.mult, ALU.add)
+            size = work.tile([P, NP], F32, name="size", tag="h", bufs=3, align_bytes=64)
+            nc.scalar.activation(size[:], rest[:], ACT.Abs, bias=shifted[:, m : m + 1])
+            cosine = work.tile([P, NP], F32, name="cosine", tag="new", bufs=3)
+            nc.scalar.activation(cosine[:], size[:], ACT.Sin, bias=-math.pi / 2)
+            result = work.tile([P, NP], F32, name="result", bufs=4)
+            engine = nc.vector if m >= SLICES - 2 else nc.gpsimd
+            engine.tensor_tensor(result[:], cosine[:], xn[m // PACK][:, m % PACK, :], ALU.mult)
+            nc.sync.dma_start(out[m * P : (m + 1) * P, :], result[:])

@@ -21,11 +21,11 @@ P = 128
 PACK = 4
 KP = P * PACK
 BANK = 512
+QUAD = 32
 PASSES1 = K // KP
 PASSES2 = H // KP
 SLICES = H // P
 TWO_PI = 2.0 * math.pi
-GROUPS = ((0, 1), (2, 3), (4, 5), (6, 7))
 
 
 def tile_list_damper_record_cosine_kernel(
@@ -37,75 +37,85 @@ def tile_list_damper_record_cosine_kernel(
         work = ctx.enter_context(tc.tile_pool(name="work", bufs=2))
         psum = ctx.enter_context(tc.psum_pool(name="psum", bufs=1))
 
+        tscale = keep.tile([P, T], U8, name="tscale", align_bytes=64)
+        nc.vector.memset(tscale[:].bitcast(I32), 0)
+        for q in range(4):
+            nc.scalar.dma_start(
+                tscale[QUAD * q : QUAD * q + 4 * PASSES1, :].bitcast(I32),
+                tab_scales[:, 4 * q : 4 * q + 4, :].bitcast(I32),
+            )
         list1 = keep.tile([P, S // 16], U16, name="list1")
         list2 = keep.tile([P, S // 16], U16, name="list2")
         list3 = keep.tile([P, NP // 16], U16, name="list3")
         nc.sync.dma_start(list1[:], offs)
 
-        tscale = keep.tile([P, T], U8, name="tscale", align_bytes=64)
-        nc.vector.memset(tscale[:].bitcast(I32), 0)
-        for q in range(4):
-            nc.scalar.dma_start(
-                tscale[32 * q : 32 * q + 4 * PASSES1, :].bitcast(I32),
-                tab_scales[:, 4 * q : 4 * q + 4, :].bitcast(I32),
-            )
+        def load_table(a):
+            table = work.tile([P, T], I32, name="table", tag="big", bufs=3, align_bytes=64)
+            nc.sync.dma_start(table[:], tab_words[a].rearrange("p t i -> p (t i)").bitcast(I32))
+            return table
+
 
         w1_codes = {}
         w1_scale = {}
 
-        def load_w1(b, a):
-            raw = work.tile([P, PACK, KP], F32, name="w1raw", bufs=3)
-            nc.sync.dma_start(
-                raw[:], w1[a * KP : (a + 1) * KP, b * KP : (b + 1) * KP].rearrange("(p i) c -> p i c", i=PACK)
-            )
-            return raw
+        def quant_w1(first, count, dealt, engine_copy):
+            width = count * P
+            for a in range(PASSES1):
+                raw = work.tile([P, PACK, width], F32, name="w1raw", bufs=3)
+                rows = w1[a * KP : (a + 1) * KP, first * P : first * P + width]
+                nc.sync.dma_start(raw[:], rows.rearrange("(p i) c -> p i c", i=PACK))
+                grouped = work.tile([P, width * PACK], BF16, name="w1bf", align_bytes=64)
+                if dealt:
+                    engine_copy(
+                        grouped[:].rearrange("p (t m i) -> p m i t", t=PACK, i=PACK),
+                        raw[:].rearrange("p i (m t) -> p m i t", t=PACK),
+                    )
+                else:
+                    engine_copy(
+                        grouped[:].rearrange("p (m t i) -> p m i t", t=4, i=PACK),
+                        raw[:].rearrange("p i (m t) -> p m i t", t=4),
+                    )
+                codes = keep.tile([P, width], U32, name="w1c%d%d" % (first, a), align_bytes=64)
+                scale = keep.tile([P, width], U8, name="w1s%d%d" % (first, a), align_bytes=64)
+                nc.vector.quantize_mx(out=codes[:].bitcast(FP8X4), scales=scale[:], in_=grouped[:])
+                for i in range(count):
+                    w1_codes[first + i, a] = codes[:, i * P : (i + 1) * P]
+                    w1_scale[first + i, a] = scale[:, i * P : (i + 1) * P]
 
-        def quant_w1(b, a, raw, engine_copy):
-            grouped = work.tile([P, KP * PACK], BF16, name="w1bf", align_bytes=64)
-            engine_copy(
-                grouped[:].rearrange("p (t m i) -> p m i t", t=PACK, i=PACK),
-                raw[:].rearrange("p i (m t) -> p m i t", t=PACK),
-            )
-            codes = keep.tile([P, KP], U32, name="w1c%d%d" % (b, a), align_bytes=64)
-            scale = keep.tile([P, KP], U8, name="w1s%d%d" % (b, a), align_bytes=64)
-            nc.vector.quantize_mx(out=codes[:].bitcast(FP8X4), scales=scale[:], in_=grouped[:])
-            w1_codes[b, a] = codes
-            w1_scale[b, a] = scale
-
-        vscale = keep.tile([P, S], U8, name="vscale", align_bytes=64)
+        quant_w1(0, 2, False, nc.vector.tensor_copy)
+        nc.sync.dma_start(list2[:], offs2)
+        tables = [load_table(a) for a in range(PASSES1)]
         vwords = []
         for a in range(PASSES1):
-            raw = load_w1(0, a)
-            table = work.tile([P, T], I32, name="big", bufs=3)
-            nc.sync.dma_start(table[:], tab_words[a].rearrange("p t i -> p (t i)").bitcast(I32))
-            quant_w1(0, a, raw, nc.vector.tensor_copy)
-            if a == 0:
-                nc.vector.tensor_copy(vscale[:], tscale[:].indirect(list1[:]))
+            table = tables[a]
             halves = []
             for u in range(2):
                 picked = keep.tile([P, BANK], U32, name="v%d%d" % (a, u), align_bytes=64)
                 nc.vector.tensor_copy(picked[:], table[:].bitcast(U32).indirect(list1[:, 32 * u : 32 * u + 32]))
                 halves.append(picked)
             vwords.append(halves)
-            if a == 1:
-                nc.sync.dma_start(list2[:], offs2)
-                nc.sync.dma_start(list3[:], offs3)
+            if a == 0:
+                vscale = work.tile([P, S], U8, name="vscale", tag="big", bufs=3, align_bytes=64)
+                nc.vector.tensor_copy(vscale[:], tscale[:].indirect(list1[:]))
 
-        page_rows = page0.rearrange("(b p t) c -> b t p c", p=P, t=PACK)
+        def slice_rows(matrix, b):
+            rows = matrix[b * KP : (b + 1) * KP, :]
+            if b == 0:
+                return rows.rearrange("(t p) c -> p t c", p=P)
+            return rows.rearrange("(p t) c -> p t c", t=PACK)
 
         def bank(i):
             return psum.tile([P, BANK], F32, name="bank%d" % i)
 
         def make_h(s):
-            b, t = divmod(s, PACK)
             h = work.tile([P, S], F32, name="h", bufs=3, align_bytes=64)
             for u in range(2):
                 acc = bank(2 * (s % 2) + u)
                 for a in range(PASSES1):
                     nc.tensor.matmul_mx(
                         out=acc[:],
-                        lhsT=w1_codes[b, a][:, t * P : (t + 1) * P].bitcast(FP8X4),
-                        lhsT_scale=w1_scale[b, a][:, t * P : (t + 1) * P],
+                        lhsT=w1_codes[s, a].bitcast(FP8X4),
+                        lhsT_scale=w1_scale[s, a],
                         rhs=vwords[a][u][:].bitcast(FP8X4),
                         rhs_scale=vscale[4 * a : P, u * BANK : (u + 1) * BANK],
                         start=(a == 0),
@@ -114,17 +124,18 @@ def tile_list_damper_record_cosine_kernel(
                 nc.scalar.copy(h[:, u * BANK : (u + 1) * BANK], acc[:])
             return h
 
-        x4 = [keep.tile([P, PACK, NP], F32, name="x4_%d" % b) for b in range(PASSES2)]
-        xn = []
+        picked_x = [keep.tile([P, PACK, NP], F32, name="picked_x%d" % b) for b in range(PASSES2)]
+        moved_x = []
         x_codes = []
         x_scale = []
 
-        def quant_x(b, engine_copy, tag):
-            grouped = work.tile([P, NP * PACK], BF16, name=tag, bufs=3, align_bytes=64)
-            engine_copy(
-                grouped[:].rearrange("p (c i t) -> p c t i", i=4, t=PACK),
-                x4[b][:].rearrange("p t (c i) -> p c t i", i=4),
-            )
+        def quant_x(b, source, shares):
+            grouped = work.tile([P, NP * PACK], BF16, name="xbf", bufs=1, align_bytes=64)
+            for engine_copy, first, last in shares:
+                engine_copy(
+                    grouped[:, PACK * first : PACK * last].rearrange("p (c i t) -> p c t i", i=4, t=PACK),
+                    source[:, :, first:last].rearrange("p t (c i) -> p c t i", i=4),
+                )
             codes = keep.tile([P, NP], U32, name="xc%d" % b, align_bytes=64)
             scale = keep.tile([P, NP], U8, name="xs%d" % b, align_bytes=64)
             nc.vector.quantize_mx(out=codes[:].bitcast(FP8X4), scales=scale[:], in_=grouped[:])
@@ -153,44 +164,52 @@ def tile_list_damper_record_cosine_kernel(
 
         floors = {}
         pages = {}
-        least_by_slice = least.rearrange("(b p t) c -> p b t c", p=P, t=PACK)
 
-        def load_group(group):
-            for s in group:
-                b, t = divmod(s, PACK)
-                page = work.tile([P, T2], F32, name="page", bufs=4)
-                nc.sync.dma_start(page[:], page_rows[b, t])
-                pages[s] = page
-            b, t = divmod(group[0], PACK)
-            floor = work.tile([P, len(group), S], F32, name="floor", align_bytes=64)
-            nc.sync.dma_start(floor[:], least_by_slice[:, b, t : t + len(group), :])
-            for i, s in enumerate(group):
-                floors[s] = floor[:, i, :]
+        def load_page(s):
+            b, t = divmod(s, PACK)
+            pages[s] = work.tile([P, T2], F32, name="page", bufs=4)
+            nc.sync.dma_start(pages[s][:], slice_rows(page0, b)[:, t, :])
 
-        groups = GROUPS
-        load_group(groups[0])
-        load_group(groups[1])
-        for a in range(PASSES1):
-            quant_w1(1, a, load_w1(1, a), nc.scalar.copy)
-        for g, group in enumerate(groups):
+        def load_floors(g):
+            b, t0 = divmod(2 * g, PACK)
+            floor = work.tile([P, 2, S], F32, name="floor")
+            nc.sync.dma_start(floor[:], slice_rows(least, b)[:, t0 : t0 + 2, :])
+            for i in range(2):
+                floors[2 * g + i] = floor[:, i, :]
+
+        pairs = SLICES // 2
+        load_page(0)
+        load_page(1)
+        load_floors(0)
+        quant_w1(2, 2, False, nc.scalar.copy)
+        load_page(2)
+        nc.sync.dma_start(list3[:], offs3)
+        load_page(3)
+        quant_w1(PACK, PACK, True, nc.scalar.copy)
+        load_floors(1)
+        for g in range(pairs):
+            group = (2 * g, 2 * g + 1)
             if g == 1:
                 nc.sync.dma_start(w2c[:].bitcast(I32), w2_words.rearrange("a p c -> p a c").bitcast(I32))
                 nc.gpsimd.memset(w2s[:].bitcast(I32), 0)
                 for q in range(4):
                     nc.sync.dma_start(
-                        w2s[32 * q : 32 * q + 4, :, :].bitcast(I32),
+                        w2s[QUAD * q : QUAD * q + 4, :, :].bitcast(I32),
                         w2_scales[:, 4 * q : 4 * q + 4, :].rearrange("a r n -> r a n").bitcast(I32),
                     )
                 with nc.allow_non_contiguous_dma(reason="one phase value a partition"):
                     nc.sync.dma_start(ph[:], phase.rearrange("(m p) -> p m", p=P))
                 nc.gpsimd.tensor_scalar(shifted[:], ph[:], 1.0, -math.pi, ALU.mult, ALU.add)
-            if g + 2 < len(groups):
-                load_group(groups[g + 2])
+            if g + 2 < pairs:
+                load_page(2 * g + 4)
+                load_page(2 * g + 5)
+                load_floors(g + 2)
             news = {}
             for s in group:
-                b, t = divmod(s, PACK)
-                if t == 0:
-                    xn.append(work.tile([P, PACK, NP], F32, name="big", bufs=3))
+                if s == 0:
+                    moved_x.append(work.tile([P, PACK, NP], F32, name="moved_x0", tag="w1raw", bufs=3))
+                if s == PACK:
+                    moved_x.append(work.tile([P, PACK, NP], F32, name="moved_x1", tag="big", bufs=3, align_bytes=64))
                 h = make_h(s)
                 new = work.tile([P, S], F32, name="new", bufs=3)
                 news[s] = new
@@ -202,33 +221,53 @@ def tile_list_damper_record_cosine_kernel(
                         )
                 else:
                     nc.vector.tensor_tensor(new[:], pages[s][:].indirect(list2[:]), h[:], ALU.add)
-            if g == len(groups) - 1:
-                quant_x(0, nc.scalar.copy, "h")
+            if g == pairs - 1:
+                quant_x(0, moved_x[0], [(nc.scalar.copy, 0, NP)])
                 for m in range(SLICES):
                     y_pass(m, 0)
             for s in group:
-                nc.vector.tensor_tensor(news[s][:], news[s][:], floors[s], ALU.max)
+                summed = news[s]
+                if s == SLICES - 2:
+                    news[s] = work.tile([P, S], F32, name="kept", tag="xbf", bufs=1, align_bytes=64)
+                nc.vector.tensor_tensor(news[s][:], summed[:], floors[s], ALU.max)
             for s in group:
                 nc.vector.tensor_copy(pages[s][:].indirect(list2[:]), news[s][:])
             for s in group:
                 b, t = divmod(s, PACK)
-                nc.vector.tensor_copy(x4[b][:, t, :], pages[s][:].indirect(list3[:]))
+                nc.vector.tensor_copy(picked_x[b][:, t, :], pages[s][:].indirect(list3[:]))
                 for q in range(4):
-                    nc.sync.dma_start(xn[b][t:P:PACK, q, :], x4[b][32 * q : 32 * q + 32, t, :])
+                    if b == 0:
+                        nc.sync.dma_start(moved_x[b][QUAD * t : QUAD * (t + 1), q, :], picked_x[b][q:P:PACK, t, :])
+                    else:
+                        nc.sync.dma_start(moved_x[b][t:P:PACK, q, :], picked_x[b][QUAD * q : QUAD * (q + 1), t, :])
 
-        quant_x(1, nc.vector.tensor_copy, "h")
+        quant_x(1, picked_x[1], [(nc.vector.tensor_copy, 0, 384), (nc.scalar.copy, 384, NP)])
+        plain_x = (picked_x[0], moved_x[1])
         for m in range(SLICES):
             y_pass(m, 1)
-            y = ybank[m]
-            turns = work.tile([P, NP], I32, name="turns", tag="w1raw", bufs=3)
-            nc.vector.tensor_scalar(turns[:], y[:], shifted[:, m : m + 1], 1.0 / TWO_PI, ALU.add, ALU.mult)
-            rest = work.tile([P, NP], F32, name="rest", tag="page", bufs=4)
-            nc.vector.scalar_tensor_tensor(rest[:], turns[:], -TWO_PI, y[:], ALU.mult, ALU.add)
-            size = work.tile([P, NP], F32, name="size", tag="h", bufs=3, align_bytes=64)
+        pieces = [(m, slice(0, NP)) for m in range(SLICES - 1)]
+        pieces.extend((SLICES - 1, slice(u * NP // 2, (u + 1) * NP // 2)) for u in range(2))
+        turns = {}
+
+        def count_turns(i):
+            m, cols = pieces[i]
+            turns[i] = work.tile([P, cols.stop - cols.start], I32, name="turns", tag="w1raw", bufs=3)
+            nc.vector.tensor_scalar(
+                turns[i][:], ybank[m][:, cols], shifted[:, m : m + 1], 1.0 / TWO_PI, ALU.add, ALU.mult
+            )
+
+        count_turns(0)
+        for i, (m, cols) in enumerate(pieces):
+            if i + 1 < len(pieces):
+                count_turns(i + 1)
+            width = cols.stop - cols.start
+            rest = work.tile([P, width], F32, name="rest", tag="page", bufs=4)
+            nc.vector.scalar_tensor_tensor(rest[:], turns[i][:], -TWO_PI, ybank[m][:, cols], ALU.mult, ALU.add)
+            size = work.tile([P, width], F32, name="size", tag="h", bufs=3, align_bytes=64)
             nc.scalar.activation(size[:], rest[:], ACT.Abs, bias=shifted[:, m : m + 1])
-            cosine = work.tile([P, NP], F32, name="cosine", tag="new", bufs=3)
+            cosine = work.tile([P, width], F32, name="cosine", tag="new", bufs=3)
             nc.scalar.activation(cosine[:], size[:], ACT.Sin, bias=-math.pi / 2)
-            result = work.tile([P, NP], F32, name="result", bufs=4)
+            result = work.tile([P, width], F32, name="result", bufs=4)
             engine = nc.vector if m >= SLICES - 2 else nc.gpsimd
-            engine.tensor_tensor(result[:], cosine[:], xn[m // PACK][:, m % PACK, :], ALU.mult)
-            nc.sync.dma_start(out[m * P : (m + 1) * P, :], result[:])
+            engine.tensor_tensor(result[:], cosine[:], plain_x[m // PACK][:, m % PACK, cols], ALU.mult)
+            nc.sync.dma_start(out[m * P : (m + 1) * P, cols], result[:])

@@ -44,6 +44,9 @@ def tile_list_damper_record_cosine_kernel(
                 tscale[QUAD * q : QUAD * q + 4 * PASSES1, :].bitcast(I32),
                 tab_scales[:, 4 * q : 4 * q + 4, :].bitcast(I32),
             )
+        warm = keep.tile([P, 16], F32, name="warm")
+        nc.gpsimd.memset(warm[:, 0:8], 0.0)
+        nc.scalar.activation(warm[:, 8:9], warm[:, 0:1], ACT.Sin)
         list1 = keep.tile([P, S // 16], U16, name="list1")
         list2 = keep.tile([P, S // 16], U16, name="list2")
         list3 = keep.tile([P, NP // 16], U16, name="list3")
@@ -245,8 +248,10 @@ def tile_list_damper_record_cosine_kernel(
         plain_x = (picked_x[0], moved_x[1])
         for m in range(SLICES):
             y_pass(m, 1)
-        pieces = [(m, slice(0, NP)) for m in range(SLICES - 1)]
-        pieces.extend((SLICES - 1, slice(u * NP // 2, (u + 1) * NP // 2)) for u in range(2))
+        pieces = []
+        for m in range(SLICES):
+            parts = 2 if m in (0, SLICES - 1) else 1
+            pieces.extend((m, slice(u * NP // parts, (u + 1) * NP // parts)) for u in range(parts))
         turns = {}
 
         def count_turns(i):
@@ -261,13 +266,13 @@ def tile_list_damper_record_cosine_kernel(
             if i + 1 < len(pieces):
                 count_turns(i + 1)
             width = cols.stop - cols.start
-            rest = work.tile([P, width], F32, name="rest", tag="page", bufs=4)
+            rest = work.tile([P, width], F32, name="rest", tag="new", bufs=3)
             nc.vector.scalar_tensor_tensor(rest[:], turns[i][:], -TWO_PI, ybank[m][:, cols], ALU.mult, ALU.add)
             size = work.tile([P, width], F32, name="size", tag="h", bufs=3, align_bytes=64)
             nc.scalar.activation(size[:], rest[:], ACT.Abs, bias=shifted[:, m : m + 1])
-            cosine = work.tile([P, width], F32, name="cosine", tag="new", bufs=3)
+            cosine = work.tile([P, width], F32, name="cosine", tag="page", bufs=4)
             nc.scalar.activation(cosine[:], size[:], ACT.Sin, bias=-math.pi / 2)
-            result = work.tile([P, width], F32, name="result", bufs=4)
-            engine = nc.vector if m >= SLICES - 2 else nc.gpsimd
+            result = work.tile([P, width], F32, name="result", bufs=8)
+            engine = nc.vector if m >= SLICES - 3 else nc.gpsimd
             engine.tensor_tensor(result[:], cosine[:], plain_x[m // PACK][:, m % PACK, cols], ALU.mult)
             nc.sync.dma_start(out[m * P : (m + 1) * P, cols], result[:])

import math
from contextlib import ExitStack

import concourse.mybir as mybir

K, T, S, H, T2, NP = 1536, 4096, 1024, 1024, 2048, 512
FLOPS = 2 * K * H * S + 2 * H * H * NP

F32 = mybir.dt.float32
BF16 = mybir.dt.bfloat16
I32 = mybir.dt.int32
U32 = mybir.dt.uint32
U16 = mybir.dt.uint16
U8 = mybir.dt.uint8
FP8X4 = mybir.dt.float8_e4m3fn_x4
FP4X4 = mybir.dt.float4_e2m1fn_x4
ALU = mybir.AluOpType
ACT = mybir.ActivationFunctionType

P = 128
PACK = 4
KP = P * PACK
BANK = 512
QUAD = 32
PASSES1 = K // KP
PASSES2 = H // KP
SLICES = H // P
TWO_PI = 2.0 * math.pi


def tile_list_damper_record_cosine_kernel(
    tc, tab_words, tab_scales, w1, w2_words, w2_scales, page0, least, phase, offs, offs2, offs3, out
):
    nc = tc.nc
    with ExitStack() as ctx:
        keep = ctx.enter_context(tc.tile_pool(name="keep", bufs=1))
        work = ctx.enter_context(tc.tile_pool(name="work", bufs=2))
        psum = ctx.enter_context(tc.psum_pool(name="psum", bufs=1))

        tscale = keep.tile([P, T], U8, name="tscale", align_bytes=64)
        nc.vector.memset(tscale[:].bitcast(I32), 0)
        for q in range(4):
            nc.scalar.dma_start(
                tscale[QUAD * q : QUAD * q + 4 * PASSES1, :].bitcast(I32),
                tab_scales[:, 4 * q : 4 * q + 4, :].bitcast(I32),
            )
        warm = keep.tile([P, 16], F32, name="warm")
        nc.gpsimd.memset(warm[:, 0:8], 0.0)
        nc.scalar.activation(warm[:, 8:9], warm[:, 0:1], ACT.Sin)
        list1 = keep.tile([P, S // 16], U16, name="list1")
        list2 = keep.tile([P, S // 16], U16, name="list2")
        list3 = keep.tile([P, NP // 16], U16, name="list3")
        nc.sync.dma_start(list1[:], offs)

        def load_table(a):
            table = work.tile([P, T], I32, name="table", tag="big", bufs=3, align_bytes=64)
            nc.sync.dma_start(table[:], tab_words[a].rearrange("p t i -> p (t i)").bitcast(I32))
            return table


        w1_codes = {}
        w1_scale = {}

        def quant_w1(first, count, dealt, engine_copy):
            width = count * P
            for a in range(PASSES1):
                raw = work.tile([P, PACK, width], F32, name="w1raw", bufs=3)
                rows = w1[a * KP : (a + 1) * KP, first * P : first * P + width]
                nc.sync.dma_start(raw[:], rows.rearrange("(p i) c -> p i c", i=PACK))
                grouped = work.tile([P, width * PACK], BF16, name="w1bf", align_bytes=64)
                if dealt:
                    engine_copy(
                        grouped[:].rearrange("p (t m i) -> p m i t", t=PACK, i=PACK),
                        raw[:].rearrange("p i (m t) -> p m i t", t=PACK),
                    )
                else:
                    engine_copy(
                        grouped[:].rearrange("p (m t i) -> p m i t", t=4, i=PACK),
                        raw[:].rearrange("p i (m t) -> p m i t", t=4),
                    )
                codes = keep.tile([P, width], U32, name="w1c%d%d" % (first, a), align_bytes=64)
                scale = keep.tile([P, width], U8, name="w1s%d%d" % (first, a), align_bytes=64)
                nc.vector.quantize_mx(out=codes[:].bitcast(FP8X4), scales=scale[:], in_=grouped[:])
                for i in range(count):
                    w1_codes[first + i, a] = codes[:, i * P : (i + 1) * P]
                    w1_scale[first + i, a] = scale[:, i * P : (i + 1) * P]

        quant_w1(0, 2, False, nc.vector.tensor_copy)
        nc.sync.dma_start(list2[:], offs2)
        tables = [load_table(a) for a in range(PASSES1)]
        vwords = []
        for a in range(PASSES1):
            table = tables[a]
            halves = []
            for u in range(2):
                picked = keep.tile([P, BANK], U32, name="v%d%d" % (a, u), align_bytes=64)
                nc.vector.tensor_copy(picked[:], table[:].bitcast(U32).indirect(list1[:, 32 * u : 32 * u + 32]))
                halves.append(picked)
            vwords.append(halves)
            if a == 0:
                vscale = work.tile([P, S], U8, name="vscale", tag="big", bufs=3, align_bytes=64)
                nc.vector.tensor_copy(vscale[:], tscale[:].indirect(list1[:]))

        def slice_rows(matrix, b):
            rows = matrix[b * KP : (b + 1) * KP, :]
            if b == 0:
                return rows.rearrange("(t p) c -> p t c", p=P)
            return rows.rearrange("(p t) c -> p t c", t=PACK)

        def bank(i):
            return psum.tile([P, BANK], F32, name="bank%d" % i)

        def make_h(s):
            h = work.tile([P, S], F32, name="h", bufs=3, align_bytes=64)
            for u in range(2):
                acc = bank(2 * (s % 2) + u)
                for a in range(PASSES1):
                    nc.tensor.matmul_mx(
                        out=acc[:],
                        lhsT=w1_codes[s, a].bitcast(FP8X4),
                        lhsT_scale=w1_scale[s, a],
                        rhs=vwords[a][u][:].bitcast(FP8X4),
                        rhs_scale=vscale[4 * a : P, u * BANK : (u + 1) * BANK],
                        start=(a == 0),
                        stop=(a == PASSES1 - 1),
                    )
                nc.scalar.copy(h[:, u * BANK : (u + 1) * BANK], acc[:])
            return h

        picked_x = [keep.tile([P, PACK, NP], F32, name="picked_x%d" % b) for b in range(PASSES2)]
        moved_x = []
        x_codes = []
        x_scale = []

        def quant_x(b, source, shares):
            grouped = work.tile([P, NP * PACK], BF16, name="xbf", bufs=1, align_bytes=64)
            for engine_copy, first, last in shares:
                engine_copy(
                    grouped[:, PACK * first : PACK * last].rearrange("p (c i t) -> p c t i", i=4, t=PACK),
                    source[:, :, first:last].rearrange("p t (c i) -> p c t i", i=4),
                )
            codes = keep.tile([P, NP], U32, name="xc%d" % b, align_bytes=64)
            scale = keep.tile([P, NP], U8, name="xs%d" % b, align_bytes=64)
            nc.vector.quantize_mx(out=codes[:].bitcast(FP8X4), scales=scale[:], in_=grouped[:])
            x_codes.append(codes)
            x_scale.append(scale)

        w2c = keep.tile([P, PASSES2, 2 * H], U8, name="w2c", align_bytes=64)
        w2s = keep.tile([P, PASSES2, H], U8, name="w2s", align_bytes=64)
        ph = keep.tile([P, SLICES], F32, name="ph")
        shifted = keep.tile([P, SLICES], F32, name="shifted")

        ybank = {}

        def y_pass(m, b):
            if b == 0:
                ybank[m] = bank((m + 4) % 8)
            nc.tensor.matmul_mx(
                out=ybank[m][:],
                lhsT=w2c[:, b, 2 * m * P : 2 * (m + 1) * P].bitcast(FP4X4),
                lhsT_scale=w2s[:, b, m * P : (m + 1) * P],
                rhs=x_codes[b][:].bitcast(FP8X4),
                rhs_scale=x_scale[b][:],
                start=(b == 0),
                stop=(b == PASSES2 - 1),
            )

        floors = {}
        pages = {}

        def load_page(s):
            b, t = divmod(s, PACK)
            pages[s] = work.tile([P, T2], F32, name="page", bufs=4)
            nc.sync.dma_start(pages[s][:], slice_rows(page0, b)[:, t, :])

        def load_floors(g):
            b, t0 = divmod(2 * g, PACK)
            floor = work.tile([P, 2, S], F32, name="floor")
            nc.sync.dma_start(floor[:], slice_rows(least, b)[:, t0 : t0 + 2, :])
            for i in range(2):
                floors[2 * g + i] = floor[:, i, :]

        pairs = SLICES // 2
        load_page(0)
        load_page(1)
        load_floors(0)
        quant_w1(2, 2, False, nc.scalar.copy)
        load_page(2)
        nc.sync.dma_start(list3[:], offs3)
        load_page(3)
        quant_w1(PACK, PACK, True, nc.scalar.copy)
        load_floors(1)
        for g in range(pairs):
            group = (2 * g, 2 * g + 1)
            if g == 1:
                nc.sync.dma_start(w2c[:].bitcast(I32), w2_words.rearrange("a p c -> p a c").bitcast(I32))
                nc.gpsimd.memset(w2s[:].bitcast(I32), 0)
                for q in range(4):
                    nc.sync.dma_start(
                        w2s[QUAD * q : QUAD * q + 4, :, :].bitcast(I32),
                        w2_scales[:, 4 * q : 4 * q + 4, :].rearrange("a r n -> r a n").bitcast(I32),
                    )
                with nc.allow_non_contiguous_dma(reason="one phase value a partition"):
                    nc.sync.dma_start(ph[:], phase.rearrange("(m p) -> p m", p=P))
                nc.gpsimd.tensor_scalar(shifted[:], ph[:], 1.0, -math.pi, ALU.mult, ALU.add)
            if g + 2 < pairs:
                load_page(2 * g + 4)
                load_page(2 * g + 5)
                load_floors(g + 2)
            news = {}
            for s in group:
                if s == 0:
                    moved_x.append(work.tile([P, PACK, NP], F32, name="moved_x0", tag="w1raw", bufs=3))
                if s == PACK:
                    moved_x.append(work.tile([P, PACK, NP], F32, name="moved_x1", tag="big", bufs=3, align_bytes=64))
                h = make_h(s)
                new = work.tile([P, S], F32, name="new", bufs=3)
                news[s] = new
                if s == 0:
                    for u in range(2):
                        cols = slice(u * BANK, (u + 1) * BANK)
                        nc.vector.tensor_tensor(
                            new[:, cols], pages[s][:].indirect(list2[:, 32 * u : 32 * u + 32]), h[:, cols], ALU.add
                        )
                else:
                    nc.vector.tensor_tensor(new[:], pages[s][:].indirect(list2[:]), h[:], ALU.add)
            if g == pairs - 1:
                quant_x(0, moved_x[0], [(nc.scalar.copy, 0, NP)])
                for m in range(SLICES):
                    y_pass(m, 0)
            for s in group:
                summed = news[s]
                if s == SLICES - 2:
                    news[s] = work.tile([P, S], F32, name="kept", tag="xbf", bufs=1, align_bytes=64)
                nc.vector.tensor_tensor(news[s][:], summed[:], floors[s], ALU.max)
            for s in group:
                nc.vector.tensor_copy(pages[s][:].indirect(list2[:]), news[s][:])
            for s in group:
                b, t = divmod(s, PACK)
                nc.vector.tensor_copy(picked_x[b][:, t, :], pages[s][:].indirect(list3[:]))
                for q in range(4):
                    if b == 0:
                        nc.sync.dma_start(moved_x[b][QUAD * t : QUAD * (t + 1), q, :], picked_x[b][q:P:PACK, t, :])
                    else:
                        nc.sync.dma_start(moved_x[b][t:P:PACK, q, :], picked_x[b][QUAD * q : QUAD * (q + 1), t, :])

        quant_x(1, picked_x[1], [(nc.vector.tensor_copy, 0, 384), (nc.scalar.copy, 384, NP)])
        plain_x = (picked_x[0], moved_x[1])
        for m in range(SLICES):
            y_pass(m, 1)
        pieces = []
        for m in range(SLICES):
            parts = 2 if m in (0, SLICES - 1) else 1
            pieces.extend((m, slice(u * NP // parts, (u + 1) * NP // parts)) for u in range(parts))
        turns = {}

        def count_turns(i):
            m, cols = pieces[i]
            turns[i] = work.tile([P, cols.stop - cols.start], I32, name="turns", tag="w1raw", bufs=3)
            nc.vector.tensor_scalar(
                turns[i][:], ybank[m][:, cols], shifted[:, m : m + 1], 1.0 / TWO_PI, ALU.add, ALU.mult
            )

        count_turns(0)
        for i, (m, cols) in enumerate(pieces):
            if i + 1 < len(pieces):
                count_turns(i + 1)
            width = cols.stop - cols.start
            rest = work.tile([P, width], F32, name="rest", tag="new", bufs=3)
            nc.vector.scalar_tensor_tensor(rest[:], turns[i][:], -TWO_PI, ybank[m][:, cols], ALU.mult, ALU.add)
            size = work.tile([P, width], F32, name="size", tag="h", bufs=3, align_bytes=64)
            nc.scalar.activation(size[:], rest[:], ACT.Abs, bias=shifted[:, m : m + 1])
            cosine = work.tile([P, width], F32, name="cosine", tag="page", bufs=4)
            nc.scalar.activation(cosine[:], size[:], ACT.Sin, bias=-math.pi / 2)
            result = work.tile([P, width], F32, name="result", bufs=8)
            engine = nc.vector if m >= SLICES - 3 else nc.gpsimd
            engine.tensor_tensor(result[:], cosine[:], plain_x[m // PACK][:, m % PACK, cols], ALU.mult)
            nc.sync.dma_start(out[m * P : (m + 1) * P, cols], result[:])
